import numpy as np
import ml_dtypes


def mxq(x, axis, fmt="e4m3"):
    dtype, down = {"e4m3": (ml_dtypes.float8_e4m3fn, 7), "e5m2": (ml_dtypes.float8_e5m2, 14)}[fmt]
    v = np.moveaxis(np.asarray(x, np.float32).astype(ml_dtypes.bfloat16).astype(np.float64), axis, -1)
    blocks = v.reshape(v.shape[:-1] + (-1, 32))
    amax = np.abs(blocks).max(-1, keepdims=True)
    byte = np.maximum(np.where(amax > 0, np.frexp(amax)[1] - 1 + 127, 0) - down, 1)
    scale = np.exp2(byte - 127.0)
    codes = (blocks / scale).astype(np.float32).astype(dtype).astype(np.float64)
    return np.moveaxis((codes * scale).reshape(v.shape), -1, axis)


WIDE = False


def mx_kscale(k):
    if not WIDE:
        return np.ones(k)
    levels = np.array([10, -10, 5, -5, 0])
    if k % 512:
        return np.exp2(np.random.permutation(np.resize(levels, k // 32))).repeat(32)
    a = np.empty((k // 512, 16))
    for p in range(k // 512):
        a[p, :8] = np.random.permutation(np.resize(levels, 8))
        for g in range(8):
            far = levels[np.abs(levels - a[p, g]) >= 10]
            a[p, g + 8] = far[np.random.randint(len(far))]
    return np.exp2(a.ravel()).repeat(32)


def f64(x):
    return np.asarray(x).astype(np.float64)


def striped(idx):
    return np.tile(idx.reshape(-1, 16).T, (8, 1)).astype(np.uint16)


def unstriped(offs):
    return offs[:16].T.reshape(-1).astype(np.int64)


E2M1 = np.array([0.0, 0.5, 1.0, 1.5, 2.0, 3.0, 4.0, 6.0, -0.0, -0.5, -1.0, -1.5, -2.0, -3.0, -4.0, -6.0])


def pack_weight(w, fmt):
    k, n = w.shape
    w = f64(np.asarray(w, np.float32).astype(ml_dtypes.bfloat16)).reshape(k // 32, 32, n)
    amax = np.abs(w).max(1)
    if fmt == "e4m3":
        byte = np.frexp(amax)[1] - 1 + 127 - 7
    else:
        mant, ex = np.frexp(amax / 6.0)
        byte = np.where(mant > 0.5, ex, ex - 1) + 127
    byte = np.clip(np.where(amax > 0, byte, 1), 1, 254)
    scaled = (w * np.exp2(127.0 - byte)[:, None, :]).reshape(k, n).astype(np.float32)
    by_word = np.ascontiguousarray(scaled.reshape(k // 512, 128, 4, n).transpose(0, 1, 3, 2))
    if fmt == "e4m3":
        words = by_word.astype(ml_dtypes.float8_e4m3fn).view(np.uint8)
    else:
        c = by_word.astype(ml_dtypes.float4_e2m1fn).view(np.uint8) & 0xF
        words = (c[..., 0::2] | (c[..., 1::2] << 4)).reshape(k // 512, 128, 2 * n)
    return np.ascontiguousarray(words), np.ascontiguousarray(byte.astype(np.uint8).reshape(k // 512, 16, n))


def unpack_weight(words, scales, fmt):
    g, _, n = scales.shape
    words = np.ascontiguousarray(words).reshape(g, 128, n, -1)
    if fmt == "e4m3":
        vals = words.view(ml_dtypes.float8_e4m3fn).astype(np.float64)
    else:
        nib = np.empty((g, 128, n, 4), np.uint8)
        nib[..., 0::2] = words & 0xF
        nib[..., 1::2] = words >> 4
        vals = E2M1[nib]
    vals = vals * np.repeat(np.exp2(scales.astype(np.float64) - 127.0), 8, axis=1)[..., None]
    return vals.transpose(0, 1, 3, 2).reshape(g * 512, n)


def gelu(v):
    return 0.5 * v * (1.0 + np.tanh(np.sqrt(2.0 / np.pi) * (v + 0.044715 * v**3)))


def striped8(idx):
    return np.concatenate([v.reshape(-1, 16).T for v in idx]).astype(np.uint16)


def unstriped8(offs):
    return np.stack([offs[16 * g:16 * g + 16].T.reshape(-1) for g in range(8)]).astype(np.int64)


def heads(xT, wgt, idx8):
    k = np.arange(xT.shape[0])
    return wgt[k // 4 % 128] * xT[k[:, None], idx8[k % 512 // 64]]


K, T, S, H, N = 1024, 2048, 1024, 1024, 512


def setup_inputs():
    n = np.random.standard_normal
    s = mx_kscale(K)[:, None]
    u = mx_kscale(H)[:, None]
    xT = n((K, T)) * s
    wgt = np.repeat(np.random.uniform(0.5, 2.0, (8, S)), 16, axis=0)
    offs = striped8(np.stack([np.random.permutation(T)[:S] for _ in range(8)]))
    w1 = n((K, H)) / np.sqrt(K) / s * u.T
    w2 = n((K, H)) / np.sqrt(K) / s
    w3 = n((H, N)) / np.sqrt(H) / u
    w2_words, w2_scales = pack_weight(w2, "e2m1")
    w3_words, w3_scales = pack_weight(w3, "e4m3")
    return {"xT": xT.astype(np.float32), "wgt": wgt.astype(np.float32),
            "offs": offs, "w1": w1.astype(np.float32),
            "w2_words": w2_words, "w2_scales": w2_scales,
            "w3_words": w3_words, "w3_scales": w3_scales,
            "bt": (0.5 * n(N)).astype(np.float32)}


def reference(xT, wgt, offs, w1, w2_words, w2_scales, w3_words, w3_scales, bt):
    xg = heads(f64(xT), f64(wgt), unstriped8(offs))
    xq = mxq(xg, 0, "e4m3")
    w1q = mxq(f64(w1), 0, "e4m3")
    w2 = unpack_weight(w2_words, w2_scales, "e2m1")
    w3 = unpack_weight(w3_words, w3_scales, "e4m3")
    a = w1q.T @ xq
    b = w2.T @ xq
    h = a / (1.0 + np.abs(b))
    hq = mxq(h, 0, "e4m3")
    y = w3.T @ hq
    return y + f64(bt)[:, None]

@@ -1,0 +1,352 @@
+from contextlib import ExitStack
+
+import concourse.mybir as mybir
+
+K, T, S, H, N = 1024, 2048, 1024, 1024, 512
+FLOPS = 2 * (2 * K * H * S + H * N * S)
+
+F32 = mybir.dt.float32
+BF16 = mybir.dt.bfloat16
+I32 = mybir.dt.int32
+U32 = mybir.dt.uint32
+U16 = mybir.dt.uint16
+U8 = mybir.dt.uint8
+FP8X4 = mybir.dt.float8_e4m3fn_x4
+FP4X4 = mybir.dt.float4_e2m1fn_x4
+ACT = mybir.ActivationFunctionType
+ALU = mybir.AluOpType
+
+P = 128
+PACK = 4
+PASS = P * PACK
+HALF = 512
+CH = 128
+SQUARE_ON_VECTOR = (13,15)
+W2_AFTER = (0, 2)
+W1_ENG = ("sv", "vv", "vv", "vv")
+IL_ENG = "svv"
+WIDE_ON_SCALAR = ()
+NARROW_ON_SCALAR = (2,)
+BB = 3
+AB = 3
+RT_BUFS = 4
+RC_BUFS = 8
+B_AT = -2
+
+
+def tile_list_haplotype_trait_predictor_kernel(
+    tc, xT, wgt, offs, w1, w2_words, w2_scales, w3_words, w3_scales, bt, out
+):
+    nc = tc.nc
+    with ExitStack() as ctx:
+        keep = ctx.enter_context(tc.tile_pool(name="keep", bufs=1))
+        big = ctx.enter_context(tc.tile_pool(name="big", bufs=8))
+        ring = ctx.enter_context(tc.tile_pool(name="ring", bufs=3))
+        psum = ctx.enter_context(tc.psum_pool(name="psum", bufs=1))
+
+        offsets = keep.tile([P, S // 16], U16, name="offsets")
+        wg = [keep.tile([P, HALF], F32, name="wg%d" % half) for half in range(2)]
+        s2raw = keep.tile([P, 2, H], U8, name="s2raw", align_bytes=64)
+        s2 = keep.tile([P, 2, H], U8, name="s2", align_bytes=64)
+        w2raw = keep.tile([P, 2, 2 * H], U8, name="w2raw", align_bytes=64)
+        w2 = keep.tile([P, 2, 2 * H], U8, name="w2", align_bytes=64)
+        w3 = keep.tile([P, 2, N], U32, name="w3", align_bytes=64)
+        s3 = keep.tile([P, 2, N], U8, name="s3", align_bytes=64)
+        bias = keep.tile([P, N // P], F32, name="bias")
+        warm = keep.tile([P, 2], F32, name="warm")
+
+        nc.gpsimd.memset(s2raw[:].rearrange("p a c -> p (a c)").bitcast(I32), 0)
+        nc.vector.memset(warm[:, 0:1], 1.0)
+        nc.scalar.activation(out=warm[:, 1:2], in_=warm[:, 0:1], func=ACT.Abs_reciprocal_sqrt)
+        nc.vector.memset(s3[:].rearrange("p a c -> p (a c)").bitcast(I32), 0)
+
+        nc.sync.dma_start(offsets[:], offs)
+        for q in range(4):
+            nc.scalar.dma_start(
+                out=s2raw[32 * q : 32 * q + 4, :, :].bitcast(I32),
+                in_=w2_scales.bitcast(I32)[:, 4 * q : 4 * q + 4, :].rearrange("a r c -> r a c"),
+            )
+        planes = []
+        w1raw = {}
+
+        def load_w1(blk, a):
+            raw = keep.tile([P, PACK, PASS], F32, name="w1raw%d%d" % (blk, a))
+            nc.sync.dma_start(
+                out=raw[:],
+                in_=w1[a * PASS : (a + 1) * PASS, blk * PASS : (blk + 1) * PASS].rearrange(
+                    "(p i) c -> p i c", i=PACK
+                ),
+            )
+            w1raw[blk, a] = raw
+
+        for a in range(2):
+            rows = xT[a * PASS : (a + 1) * PASS, :].rearrange("(p i) t -> p i t", i=PACK)
+            for i in range(PACK):
+                plane = big.tile([P, T], F32, name="plane", tag="big")
+                nc.sync.dma_start(out=plane[:], in_=rows[:, i, :])
+                planes.append(plane)
+                if (a, i) == (0, 0):
+                    for half in range(2):
+                        cols = slice(half * HALF, (half + 1) * HALF)
+                        nc.sync.dma_start(out=wg[half][:], in_=wgt[:, cols])
+                if (a, i) == W2_AFTER:
+                    nc.sync.dma_start(
+                        out=w2raw[:].bitcast(I32), in_=w2_words.bitcast(I32).rearrange("a p c -> p a c")
+                    )
+        load_w1(0, 0)
+        load_w1(0, 1)
+        load_w1(1, 0)
+        load_w1(1, 1)
+        nc.sync.dma_start(
+            out=w3[:].bitcast(I32), in_=w3_words.rearrange("a p n t -> p a (n t)").bitcast(I32)
+        )
+        for q in range(4):
+            nc.sync.dma_start(
+                out=s3[32 * q : 32 * q + 4, :, :].bitcast(I32),
+                in_=w3_scales.bitcast(I32)[:, 4 * q : 4 * q + 4, :].rearrange("a r c -> r a c"),
+            )
+        with nc.allow_non_contiguous_dma(reason="one bias value a partition"):
+            nc.sync.dma_start(out=bias[:], in_=bt.rearrange("(c p) -> p c", p=P))
+
+        def deal_w2(blk):
+            cols = slice(blk * PASS, (blk + 1) * PASS)
+            nc.vector.tensor_copy(
+                out=w2[:].bitcast(U16)[:, :, cols].rearrange("p a (t m) -> p a t m", t=PACK),
+                in_=w2raw[:].bitcast(U16)[:, :, cols].rearrange("p a (m t) -> p a t m", t=PACK),
+            )
+            nc.vector.tensor_copy(
+                out=s2[:, :, cols].rearrange("p a (t m) -> p a t m", t=PACK),
+                in_=s2raw[:, :, cols].rearrange("p a (m t) -> p a t m", t=PACK),
+            )
+
+        xq = [keep.tile([P, S], U32, name="xq%d" % a, align_bytes=64) for a in range(2)]
+        xs = [keep.tile([P, S], U8, name="xs%d" % a, align_bytes=64) for a in range(2)]
+        picked = {}
+
+        def gather(a, i, half, j0=0, n=HALF):
+            if (a, half) not in picked:
+                tag = "picked1" if a == 1 else "picked0%d" % half
+                picked[a, half] = keep.tile([P, PACK, HALF], F32, name="picked", tag=tag)
+            j = half * HALF + j0
+            nc.vector.tensor_tensor(
+                picked[a, half][:, i, j0 : j0 + n],
+                planes[PACK * a + i][:].indirect(offsets[:, j // 16 : (j + n) // 16]),
+                wg[half][:, j0 : j0 + n],
+                ALU.mult,
+            )
+
+        def weave_x(a, half, j0, n, eng="s"):
+            xb = ring.tile([P, n, PACK], BF16, name="xb", tag="xb", align_bytes=64)
+            (nc.scalar.copy if eng == "s" else nc.vector.tensor_copy)(
+                out=xb[:].rearrange("p (c e) i -> p c i e", e=2),
+                in_=picked[a, half][:, :, j0 : j0 + n].rearrange("p i (c e) -> p c i e", e=2),
+            )
+            return xb
+
+        def quant_x(a, half, j0, n, xb):
+            j = half * HALF + j0
+            quant(xb, xq[a][:, j : j + n], xs[a][:, j : j + n])
+
+        def quant(src, codes, scales):
+            nc.vector.quantize_mx(
+                out=codes.bitcast(FP8X4), scales=scales, in_=src[:].rearrange("p c i -> p (c i)")
+            )
+
+        w1q = {}
+        w1s = {}
+
+        def cast_w1(blk, a, eng):
+            wb = ring.tile([P, PASS, PACK], BF16, name="wb", tag="wb", bufs=2, align_bytes=64)
+            for u in range(2):
+                dst = wb[:].rearrange("p (u e m) i -> p u m i e", u=2, e=2)[:, u]
+                src = w1raw[blk, a][:].rearrange("p i (m u e) -> p u m i e", u=2, e=2)[:, u]
+                if eng[u] == "s":
+                    nc.scalar.copy(out=dst, in_=src)
+                else:
+                    nc.vector.tensor_copy(out=dst, in_=src)
+            return wb
+
+        def quant_w1(blk, a, wb):
+            w1q[blk, a] = keep.tile([P, PASS], U32, name="w1q%d%d" % (blk, a), align_bytes=64)
+            w1s[blk, a] = keep.tile([P, PASS], U8, name="w1s%d%d" % (blk, a), align_bytes=64)
+            quant(wb, w1q[blk, a][:], w1s[blk, a][:])
+
+        for i in range(PACK):
+            gather(0, i, 0)
+            gather(0, i, 1)
+        xb00 = weave_x(0, 0, 0, HALF)
+        xb01 = weave_x(0, 1, 0, HALF)
+        for i in range(PACK - 1):
+            gather(1, i, 0)
+        gather(1, PACK - 1, 0, 0, 256)
+        gather(1, PACK - 1, 0, 256, 256)
+        quant_x(0, 0, 0, HALF, xb00)
+        deal_w2(0)
+        xa = weave_x(1, 0, 0, 256, IL_ENG[0])
+        xb = weave_x(1, 0, 256, 256, IL_ENG[1])
+        quant_x(1, 0, 0, 256, xa)
+        quant_x(1, 0, 256, 256, xb)
+        def second_half():
+            for i in range(PACK):
+                gather(1, i, 1)
+            quant_x(1, 1, 0, HALF, weave_x(1, 1, 0, HALF, IL_ENG[2]))
+
+        if B_AT == -2:
+            second_half()
+        quant_w1(0, 0, cast_w1(0, 0, W1_ENG[0]))
+        if B_AT == -1:
+            second_half()
+        quant_w1(0, 1, cast_w1(0, 1, W1_ENG[1]))
+        deal_w2(1)
+        quant_x(0, 1, 0, HALF, xb01)
+
+        hq = [keep.tile([P, S], U32, name="hq%d" % b, align_bytes=64) for b in range(2)]
+        hs = [keep.tile([P, S], U8, name="hs%d" % b, align_bytes=64) for b in range(2)]
+        groups = [(blk, half) for half in range(2) for blk in range(2)]
+        mags = {}
+
+        def damp(g, t):
+            blk, half = groups[g]
+            if t == 0:
+                mags[g] = big.tile([P, PACK, HALF], F32, name="mag", tag="big")
+            cols = slice(half * HALF, (half + 1) * HALF)
+            bank = psum.tile([P, HALF], F32, name="bbank", tag="bbank", bufs=BB)
+            c0 = blk * PASS + t * P
+            for a in range(2):
+                nc.tensor.matmul_mx(
+                    out=bank[:],
+                    lhsT=w2[:, a, 2 * c0 : 2 * (c0 + P)].bitcast(FP4X4),
+                    lhsT_scale=s2[:, a, c0 : c0 + P],
+                    rhs=xq[a][:, cols].bitcast(FP8X4),
+                    rhs_scale=xs[a][:, cols],
+                    start=(a == 0),
+                    stop=(a == 1),
+                )
+            nc.scalar.activation(out=mags[g][:, t, :], in_=bank[:], func=ACT.Abs)
+
+        def root(g, c):
+            rt = ring.tile([P, PACK, CH], F32, name="rt", tag="rt", bufs=RT_BUFS)
+            nc.scalar.activation(
+                out=rt[:], in_=mags[g][:, :, c * CH : (c + 1) * CH], func=ACT.Abs_reciprocal_sqrt, bias=1.0
+            )
+            return rt
+
+        def square(rt, on_vector):
+            rc = ring.tile([P, PACK, CH], F32, name="rc", tag="rc", bufs=RC_BUFS)
+            if on_vector:
+                nc.vector.tensor_tensor(rc[:], rt[:], rt[:], ALU.mult)
+            else:
+                nc.scalar.activation(out=rc[:], in_=rt[:], func=ACT.Square)
+            return rc
+
+        def signal(g, c, rc):
+            blk, half = groups[g]
+            j0 = half * HALF + c * CH
+            bank = psum.tile([P, PACK, CH], F32, name="abank", tag="abank", bufs=AB)
+            for t in range(PACK):
+                for a in range(2):
+                    nc.tensor.matmul_mx(
+                        out=bank[:, t, :],
+                        lhsT=w1q[blk, a][:, t * P : (t + 1) * P].bitcast(FP8X4),
+                        lhsT_scale=w1s[blk, a][:, t * P : (t + 1) * P],
+                        rhs=xq[a][:, j0 : j0 + CH].bitcast(FP8X4),
+                        rhs_scale=xs[a][:, j0 : j0 + CH],
+                        start=(a == 0),
+                        stop=(a == 1),
+                    )
+            hb = ring.tile([P, CH, PACK], BF16, name="hb", tag="hb", align_bytes=64)
+            nc.vector.tensor_tensor(
+                hb[:].rearrange("p (c e) t -> p c t e", e=2),
+                bank[:].rearrange("p t (c e) -> p c t e", e=2),
+                rc[:].rearrange("p t (c e) -> p c t e", e=2),
+                ALU.mult,
+            )
+            return hb
+
+        def quant_h(g, c, hb):
+            blk, half = groups[g]
+            j0 = half * HALF + c * CH
+            quant(hb, hq[blk][:, j0 : j0 + CH], hs[blk][:, j0 : j0 + CH])
+
+        def traits_wide(j0, nt):
+            bank = psum.tile([P, HALF], F32, name="ybank", tag="ybank", bufs=2)
+            for b in range(2):
+                nc.tensor.matmul_mx(
+                    out=bank[:],
+                    lhsT=w3[:, b, nt * P : (nt + 1) * P].bitcast(FP8X4),
+                    lhsT_scale=s3[:, b, nt * P : (nt + 1) * P],
+                    rhs=hq[b][:, j0 : j0 + HALF].bitcast(FP8X4),
+                    rhs_scale=hs[b][:, j0 : j0 + HALF],
+                    start=(b == 0),
+                    stop=(b == 1),
+                )
+            res = ring.tile([P, HALF], F32, name="res", tag="res")
+            if nt in WIDE_ON_SCALAR:
+                nc.scalar.activation(out=res[:], in_=bank[:], func=ACT.Identity, bias=bias[:, nt : nt + 1])
+            else:
+                nc.vector.tensor_scalar(
+                    out=res[:], in0=bank[:], scalar1=bias[:, nt : nt + 1], scalar2=None, op0=ALU.add
+                )
+            nc.sync.dma_start(out=out[nt * P : (nt + 1) * P, j0 : j0 + HALF], in_=res[:])
+
+        def traits_narrow(j0):
+            bank = psum.tile([P, N // P, CH], F32, name="ybank", tag="ybank", bufs=2)
+            for nt in range(N // P):
+                for b in range(2):
+                    nc.tensor.matmul_mx(
+                        out=bank[:, nt, :],
+                        lhsT=w3[:, b, nt * P : (nt + 1) * P].bitcast(FP8X4),
+                        lhsT_scale=s3[:, b, nt * P : (nt + 1) * P],
+                        rhs=hq[b][:, j0 : j0 + CH].bitcast(FP8X4),
+                        rhs_scale=hs[b][:, j0 : j0 + CH],
+                        start=(b == 0),
+                        stop=(b == 1),
+                    )
+            res = ring.tile([P, N // P, CH], F32, name="res", tag="res")
+            if (j0 - HALF) // CH in NARROW_ON_SCALAR:
+                for nt in range(N // P):
+                    nc.scalar.activation(
+                        out=res[:, nt, :], in_=bank[:, nt, :], func=ACT.Identity, bias=bias[:, nt : nt + 1]
+                    )
+            else:
+                nc.vector.tensor_tensor(
+                    res[:], bank[:], bias[:].unsqueeze(2).to_broadcast([P, N // P, CH]), ALU.add
+                )
+            nc.sync.dma_start(
+                out=out[:, j0 : j0 + CH].rearrange("(c p) j -> p c j", p=P), in_=res[:]
+            )
+
+        for t in range(PACK):
+            damp(0, t)
+        steps = [(g, c) for g in range(4) for c in range(4)]
+        rts = {0: root(0, 0)}
+        rcs = {0: square(rts[0], False)}
+        rts[1] = root(0, 1)
+        hbs = {}
+        wbs = {}
+        for n, (g, c) in enumerate(steps):
+            if n in (0, 1):
+                wbs[n] = cast_w1(1, n, W1_ENG[2 + n])
+            if n in (1, 2):
+                quant_w1(1, n - 1, wbs[n - 1])
+            if n == B_AT:
+                second_half()
+            if g + 1 < 4:
+                damp(g + 1, c)
+            if n + 1 < len(steps) and (c < 3 or g == 3):
+                rcs[n + 1] = square(rts[n + 1], n + 1 in SQUARE_ON_VECTOR)
+            if n + 2 < len(steps) and (c < 2 or g == 3):
+                rts[n + 2] = root(*steps[n + 2])
+            if c == 3 and g < 3:
+                rts[n + 1] = root(*steps[n + 1])
+                rts[n + 2] = root(*steps[n + 2])
+                rcs[n + 1] = square(rts[n + 1], n + 1 in SQUARE_ON_VECTOR)
+            hbs[n] = signal(g, c, rcs[n])
+            if n >= 1:
+                quant_h(steps[n - 1][0], steps[n - 1][1], hbs[n - 1])
+            if g == 2:
+                traits_wide(0, c)
+            if g == 3 and c >= 1:
+                traits_narrow(HALF + (c - 1) * CH)
+        quant_h(3, 3, hbs[15])
+        traits_narrow(HALF + 3 * CH)

@@ -21,17 +21,22 @@ PACK = 4
 PASS = P * PACK
 HALF = 512
 CH = 128
-SQUARE_ON_VECTOR = (13,15)
+SQUARE_ON_VECTOR = (7,)
 W2_AFTER = (0, 2)
 W1_ENG = ("sv", "vv", "vv", "vv")
-IL_ENG = "svv"
+IL_ENG = "ssvvv"
 WIDE_ON_SCALAR = ()
-NARROW_ON_SCALAR = (2,)
-BB = 3
-AB = 3
-RT_BUFS = 4
-RC_BUFS = 8
-B_AT = -2
+NARROW = "ssbb"
+WIDTH = (128, 256, 256, 128)
+RES_BUFS = 4
+BB = 4
+XB = 3
+W11_AT = -1
+AB = 2
+RT_BUFS = 3
+RC_BUFS = 6
+B_AT = 0
+HOLD = "picked10"
 
 
 def tile_list_haplotype_trait_predictor_kernel(
@@ -47,9 +52,9 @@ def tile_list_haplotype_trait_predictor_kernel(
         offsets = keep.tile([P, S // 16], U16, name="offsets")
         wg = [keep.tile([P, HALF], F32, name="wg%d" % half) for half in range(2)]
         s2raw = keep.tile([P, 2, H], U8, name="s2raw", align_bytes=64)
-        s2 = keep.tile([P, 2, H], U8, name="s2", align_bytes=64)
-        w2raw = keep.tile([P, 2, 2 * H], U8, name="w2raw", align_bytes=64)
-        w2 = keep.tile([P, 2, 2 * H], U8, name="w2", align_bytes=64)
+        s2 = [keep.tile([P, 2, PASS], U8, name="s2_%d" % b, align_bytes=64) for b in range(2)]
+        w2raw = [keep.tile([P, 2, 2 * PASS], U8, name="w2raw%d" % b, align_bytes=64) for b in range(2)]
+        w2 = [keep.tile([P, 2, 2 * PASS], U8, name="w2_%d" % b, align_bytes=64) for b in range(2)]
         w3 = keep.tile([P, 2, N], U32, name="w3", align_bytes=64)
         s3 = keep.tile([P, 2, N], U8, name="s3", align_bytes=64)
         bias = keep.tile([P, N // P], F32, name="bias")
@@ -61,16 +66,28 @@ def tile_list_haplotype_trait_predictor_kernel(
         nc.vector.memset(s3[:].rearrange("p a c -> p (a c)").bitcast(I32), 0)
 
         nc.sync.dma_start(offsets[:], offs)
-        for q in range(4):
-            nc.scalar.dma_start(
-                out=s2raw[32 * q : 32 * q + 4, :, :].bitcast(I32),
-                in_=w2_scales.bitcast(I32)[:, 4 * q : 4 * q + 4, :].rearrange("a r c -> r a c"),
+
+        def load_s2():
+            for q in range(4):
+                nc.sync.dma_start(
+                    out=s2raw[32 * q : 32 * q + 4, :, :].bitcast(I32),
+                    in_=w2_scales.bitcast(I32)[:, 4 * q : 4 * q + 4, :].rearrange("a r c -> r a c"),
+                )
+
+        def load_w2(blk):
+            cols = slice(blk * PASS // 2, (blk + 1) * PASS // 2)
+            nc.sync.dma_start(
+                out=w2raw[blk][:].bitcast(I32),
+                in_=w2_words.bitcast(I32)[:, :, cols].rearrange("a p c -> p a c"),
             )
+
+        nc.sync.dma_start(out=wg[0][:], in_=wgt[:, 0:HALF])
+        load_s2()
         planes = []
         w1raw = {}
 
         def load_w1(blk, a):
-            raw = keep.tile([P, PACK, PASS], F32, name="w1raw%d%d" % (blk, a))
+            raw = keep.tile([P, PACK, PASS], F32, name="w1raw", tag="w1raw%d%d" % (blk, a))
             nc.sync.dma_start(
                 out=raw[:],
                 in_=w1[a * PASS : (a + 1) * PASS, blk * PASS : (blk + 1) * PASS].rearrange(
@@ -86,14 +103,11 @@ def tile_list_haplotype_trait_predictor_kernel(
                 nc.sync.dma_start(out=plane[:], in_=rows[:, i, :])
                 planes.append(plane)
                 if (a, i) == (0, 0):
-                    for half in range(2):
-                        cols = slice(half * HALF, (half + 1) * HALF)
-                        nc.sync.dma_start(out=wg[half][:], in_=wgt[:, cols])
+                    nc.sync.dma_start(out=wg[1][:], in_=wgt[:, HALF:S])
                 if (a, i) == W2_AFTER:
-                    nc.sync.dma_start(
-                        out=w2raw[:].bitcast(I32), in_=w2_words.bitcast(I32).rearrange("a p c -> p a c")
-                    )
+                    load_w2(0)
         load_w1(0, 0)
+        load_w2(1)
         load_w1(0, 1)
         load_w1(1, 0)
         load_w1(1, 1)
@@ -109,14 +123,15 @@ def tile_list_haplotype_trait_predictor_kernel(
             nc.sync.dma_start(out=bias[:], in_=bt.rearrange("(c p) -> p c", p=P))
 
         def deal_w2(blk):
-            cols = slice(blk * PASS, (blk + 1) * PASS)
             nc.vector.tensor_copy(
-                out=w2[:].bitcast(U16)[:, :, cols].rearrange("p a (t m) -> p a t m", t=PACK),
-                in_=w2raw[:].bitcast(U16)[:, :, cols].rearrange("p a (m t) -> p a t m", t=PACK),
+                out=w2[blk][:].bitcast(U16).rearrange("p a (t m) -> p a t m", t=PACK),
+                in_=w2raw[blk][:].bitcast(U16).rearrange("p a (m t) -> p a t m", t=PACK),
             )
+
+        def deal_s2(blk):
             nc.vector.tensor_copy(
-                out=s2[:, :, cols].rearrange("p a (t m) -> p a t m", t=PACK),
-                in_=s2raw[:, :, cols].rearrange("p a (m t) -> p a t m", t=PACK),
+                out=s2[blk][:].rearrange("p a (t m) -> p a t m", t=PACK),
+                in_=s2raw[:, :, blk * PASS : (blk + 1) * PASS].rearrange("p a (m t) -> p a t m", t=PACK),
             )
 
         xq = [keep.tile([P, S], U32, name="xq%d" % a, align_bytes=64) for a in range(2)]
@@ -125,7 +140,7 @@ def tile_list_haplotype_trait_predictor_kernel(
 
         def gather(a, i, half, j0=0, n=HALF):
             if (a, half) not in picked:
-                tag = "picked1" if a == 1 else "picked0%d" % half
+                tag = HOLD if (a, half) == (1, 1) else "picked%d%d" % (a, half)
                 picked[a, half] = keep.tile([P, PACK, HALF], F32, name="picked", tag=tag)
             j = half * HALF + j0
             nc.vector.tensor_tensor(
@@ -136,7 +151,7 @@ def tile_list_haplotype_trait_predictor_kernel(
             )
 
         def weave_x(a, half, j0, n, eng="s"):
-            xb = ring.tile([P, n, PACK], BF16, name="xb", tag="xb", align_bytes=64)
+            xb = ring.tile([P, n, PACK], BF16, name="xb", tag="xb", bufs=XB, align_bytes=64)
             (nc.scalar.copy if eng == "s" else nc.vector.tensor_copy)(
                 out=xb[:].rearrange("p (c e) i -> p c i e", e=2),
                 in_=picked[a, half][:, :, j0 : j0 + n].rearrange("p i (c e) -> p c i e", e=2),
@@ -171,6 +186,8 @@ def tile_list_haplotype_trait_predictor_kernel(
             w1s[blk, a] = keep.tile([P, PASS], U8, name="w1s%d%d" % (blk, a), align_bytes=64)
             quant(wb, w1q[blk, a][:], w1s[blk, a][:])
 
+        deal_s2(0)
+        deal_s2(1)
         for i in range(PACK):
             gather(0, i, 0)
             gather(0, i, 1)
@@ -178,18 +195,17 @@ def tile_list_haplotype_trait_predictor_kernel(
         xb01 = weave_x(0, 1, 0, HALF)
         for i in range(PACK - 1):
             gather(1, i, 0)
-        gather(1, PACK - 1, 0, 0, 256)
-        gather(1, PACK - 1, 0, 256, 256)
         quant_x(0, 0, 0, HALF, xb00)
         deal_w2(0)
-        xa = weave_x(1, 0, 0, 256, IL_ENG[0])
-        xb = weave_x(1, 0, 256, 256, IL_ENG[1])
-        quant_x(1, 0, 0, 256, xa)
-        quant_x(1, 0, 256, 256, xb)
+        for c in range(4):
+            gather(1, PACK - 1, 0, c * CH, CH)
+            quant_x(1, 0, c * CH, CH, weave_x(1, 0, c * CH, CH, IL_ENG[c]))
+        deal_w2(1)
+
         def second_half():
             for i in range(PACK):
                 gather(1, i, 1)
-            quant_x(1, 1, 0, HALF, weave_x(1, 1, 0, HALF, IL_ENG[2]))
+            quant_x(1, 1, 0, HALF, weave_x(1, 1, 0, HALF, IL_ENG[4]))
 
         if B_AT == -2:
             second_half()
@@ -197,7 +213,8 @@ def tile_list_haplotype_trait_predictor_kernel(
         if B_AT == -1:
             second_half()
         quant_w1(0, 1, cast_w1(0, 1, W1_ENG[1]))
-        deal_w2(1)
+        if B_AT == 0:
+            second_half()
         quant_x(0, 1, 0, HALF, xb01)
 
         hq = [keep.tile([P, S], U32, name="hq%d" % b, align_bytes=64) for b in range(2)]
@@ -208,15 +225,15 @@ def tile_list_haplotype_trait_predictor_kernel(
         def damp(g, t):
             blk, half = groups[g]
             if t == 0:
-                mags[g] = big.tile([P, PACK, HALF], F32, name="mag", tag="big")
+                mags[g] = keep.tile([P, PACK, HALF], F32, name="mag", tag="picked00")
             cols = slice(half * HALF, (half + 1) * HALF)
             bank = psum.tile([P, HALF], F32, name="bbank", tag="bbank", bufs=BB)
-            c0 = blk * PASS + t * P
+            c0 = t * P
             for a in range(2):
                 nc.tensor.matmul_mx(
                     out=bank[:],
-                    lhsT=w2[:, a, 2 * c0 : 2 * (c0 + P)].bitcast(FP4X4),
-                    lhsT_scale=s2[:, a, c0 : c0 + P],
+                    lhsT=w2[blk][:, a, 2 * c0 : 2 * (c0 + P)].bitcast(FP4X4),
+                    lhsT_scale=s2[blk][:, a, c0 : c0 + P],
                     rhs=xq[a][:, cols].bitcast(FP8X4),
                     rhs_scale=xs[a][:, cols],
                     start=(a == 0),
@@ -224,49 +241,68 @@ def tile_list_haplotype_trait_predictor_kernel(
                 )
             nc.scalar.activation(out=mags[g][:, t, :], in_=bank[:], func=ACT.Abs)
 
-        def root(g, c):
-            rt = ring.tile([P, PACK, CH], F32, name="rt", tag="rt", bufs=RT_BUFS)
+        def damp_first(c):
+            if c == 0:
+                mags[0] = keep.tile([P, PACK, HALF], F32, name="mag", tag="picked00")
+            cols = slice(c * CH, (c + 1) * CH)
+            bank = psum.tile([P, PACK, CH], F32, name="bbank", tag="bbank", bufs=BB)
+            for a in range(2):
+                for t in range(PACK):
+                    nc.tensor.matmul_mx(
+                        out=bank[:, t, :],
+                        lhsT=w2[0][:, a, 2 * t * P : 2 * (t + 1) * P].bitcast(FP4X4),
+                        lhsT_scale=s2[0][:, a, t * P : (t + 1) * P],
+                        rhs=xq[a][:, cols].bitcast(FP8X4),
+                        rhs_scale=xs[a][:, cols],
+                        start=(a == 0 and t == 0),
+                        stop=(a == 1 and t == PACK - 1),
+                    )
+            nc.scalar.activation(out=mags[0][:, :, cols], in_=bank[:], func=ACT.Abs)
+
+        def root(g, j0, n):
+            rt = ring.tile([P, PACK, n], F32, name="rt", tag="rt", bufs=RT_BUFS)
             nc.scalar.activation(
-                out=rt[:], in_=mags[g][:, :, c * CH : (c + 1) * CH], func=ACT.Abs_reciprocal_sqrt, bias=1.0
+                out=rt[:], in_=mags[g][:, :, j0 : j0 + n], func=ACT.Abs_reciprocal_sqrt, bias=1.0
             )
             return rt
 
-        def square(rt, on_vector):
-            rc = ring.tile([P, PACK, CH], F32, name="rc", tag="rc", bufs=RC_BUFS)
+        def square(rt, n, on_vector):
+            rc = ring.tile([P, PACK, n], F32, name="rc", tag="rc", bufs=RC_BUFS)
             if on_vector:
                 nc.vector.tensor_tensor(rc[:], rt[:], rt[:], ALU.mult)
             else:
                 nc.scalar.activation(out=rc[:], in_=rt[:], func=ACT.Square)
             return rc
 
-        def signal(g, c, rc):
+        def signal(g, j0, n, rc):
             blk, half = groups[g]
-            j0 = half * HALF + c * CH
-            bank = psum.tile([P, PACK, CH], F32, name="abank", tag="abank", bufs=AB)
-            for t in range(PACK):
-                for a in range(2):
-                    nc.tensor.matmul_mx(
-                        out=bank[:, t, :],
-                        lhsT=w1q[blk, a][:, t * P : (t + 1) * P].bitcast(FP8X4),
-                        lhsT_scale=w1s[blk, a][:, t * P : (t + 1) * P],
-                        rhs=xq[a][:, j0 : j0 + CH].bitcast(FP8X4),
-                        rhs_scale=xs[a][:, j0 : j0 + CH],
-                        start=(a == 0),
-                        stop=(a == 1),
-                    )
-            hb = ring.tile([P, CH, PACK], BF16, name="hb", tag="hb", align_bytes=64)
-            nc.vector.tensor_tensor(
-                hb[:].rearrange("p (c e) t -> p c t e", e=2),
-                bank[:].rearrange("p t (c e) -> p c t e", e=2),
-                rc[:].rearrange("p t (c e) -> p c t e", e=2),
-                ALU.mult,
-            )
+            hb = ring.tile([P, n, PACK], BF16, name="hb", tag="hb", align_bytes=64)
+            for c0 in range(0, n, CH):
+                j = half * HALF + j0 + c0
+                bank = psum.tile([P, PACK, CH], F32, name="abank", tag="abank", bufs=AB)
+                for t in range(PACK):
+                    for a in range(2):
+                        nc.tensor.matmul_mx(
+                            out=bank[:, t, :],
+                            lhsT=w1q[blk, a][:, t * P : (t + 1) * P].bitcast(FP8X4),
+                            lhsT_scale=w1s[blk, a][:, t * P : (t + 1) * P],
+                            rhs=xq[a][:, j : j + CH].bitcast(FP8X4),
+                            rhs_scale=xs[a][:, j : j + CH],
+                            start=(a == 0),
+                            stop=(a == 1),
+                        )
+                nc.vector.tensor_tensor(
+                    hb[:, c0 : c0 + CH, :].rearrange("p (c e) t -> p c t e", e=2),
+                    bank[:].rearrange("p t (c e) -> p c t e", e=2),
+                    rc[:, :, c0 : c0 + CH].rearrange("p t (c e) -> p c t e", e=2),
+                    ALU.mult,
+                )
             return hb
 
-        def quant_h(g, c, hb):
+        def quant_h(g, j0, n, hb):
             blk, half = groups[g]
-            j0 = half * HALF + c * CH
-            quant(hb, hq[blk][:, j0 : j0 + CH], hs[blk][:, j0 : j0 + CH])
+            j = half * HALF + j0
+            quant(hb, hq[blk][:, j : j + n], hs[blk][:, j : j + n])
 
         def traits_wide(j0, nt):
             bank = psum.tile([P, HALF], F32, name="ybank", tag="ybank", bufs=2)
@@ -280,7 +316,7 @@ def tile_list_haplotype_trait_predictor_kernel(
                     start=(b == 0),
                     stop=(b == 1),
                 )
-            res = ring.tile([P, HALF], F32, name="res", tag="res")
+            res = big.tile([P, HALF], F32, name="res", tag="big")
             if nt in WIDE_ON_SCALAR:
                 nc.scalar.activation(out=res[:], in_=bank[:], func=ACT.Identity, bias=bias[:, nt : nt + 1])
             else:
@@ -289,64 +325,78 @@ def tile_list_haplotype_trait_predictor_kernel(
                 )
             nc.sync.dma_start(out=out[nt * P : (nt + 1) * P, j0 : j0 + HALF], in_=res[:])
 
-        def traits_narrow(j0):
-            bank = psum.tile([P, N // P, CH], F32, name="ybank", tag="ybank", bufs=2)
-            for nt in range(N // P):
-                for b in range(2):
+        def traits_narrow(j0, nt0, count, tag, bufs, on_scalar):
+            bank = psum.tile([P, count, CH], F32, name="ybank", tag=tag, bufs=bufs)
+            for b in range(2):
+                for k in range(count):
+                    nt = nt0 + k
                     nc.tensor.matmul_mx(
-                        out=bank[:, nt, :],
+                        out=bank[:, k, :],
                         lhsT=w3[:, b, nt * P : (nt + 1) * P].bitcast(FP8X4),
                         lhsT_scale=s3[:, b, nt * P : (nt + 1) * P],
                         rhs=hq[b][:, j0 : j0 + CH].bitcast(FP8X4),
                         rhs_scale=hs[b][:, j0 : j0 + CH],
-                        start=(b == 0),
-                        stop=(b == 1),
+                        start=(b == 0 and k == 0),
+                        stop=(b == 1 and k == count - 1),
                     )
-            res = ring.tile([P, N // P, CH], F32, name="res", tag="res")
-            if (j0 - HALF) // CH in NARROW_ON_SCALAR:
-                for nt in range(N // P):
+            res = big.tile([P, count, CH], F32, name="res", tag="big")
+            if on_scalar:
+                for k in range(count):
                     nc.scalar.activation(
-                        out=res[:, nt, :], in_=bank[:, nt, :], func=ACT.Identity, bias=bias[:, nt : nt + 1]
+                        out=res[:, k, :], in_=bank[:, k, :], func=ACT.Identity, bias=bias[:, nt0 + k : nt0 + k + 1]
                     )
             else:
                 nc.vector.tensor_tensor(
-                    res[:], bank[:], bias[:].unsqueeze(2).to_broadcast([P, N // P, CH]), ALU.add
+                    res[:], bank[:], bias[:, nt0 : nt0 + count].unsqueeze(2).to_broadcast([P, count, CH]), ALU.add
                 )
-            nc.sync.dma_start(
-                out=out[:, j0 : j0 + CH].rearrange("(c p) j -> p c j", p=P), in_=res[:]
+            (nc.scalar if on_scalar else nc.sync).dma_start(
+                out=out[nt0 * P : (nt0 + count) * P, j0 : j0 + CH].rearrange("(c p) j -> p c j", p=P), in_=res[:]
             )
 
-        for t in range(PACK):
-            damp(0, t)
-        steps = [(g, c) for g in range(4) for c in range(4)]
-        rts = {0: root(0, 0)}
-        rcs = {0: square(rts[0], False)}
-        rts[1] = root(0, 1)
+        def traits_chunk(c):
+            j0 = HALF + c * CH
+            if NARROW[c] == "b":
+                traits_narrow(j0, 0, 2, "ybank", 2, False)
+                traits_narrow(j0, 2, 2, "bbank", BB, True)
+            else:
+                traits_narrow(j0, 0, 4, "ybank", 2, NARROW[c] == "s")
+
+        steps = [(g, j0, WIDTH[g]) for g in range(4) for j0 in range(0, HALF, WIDTH[g])]
+        rts = {}
+        rcs = {}
         hbs = {}
-        wbs = {}
-        for n, (g, c) in enumerate(steps):
-            if n in (0, 1):
-                wbs[n] = cast_w1(1, n, W1_ENG[2 + n])
-            if n in (1, 2):
-                quant_w1(1, n - 1, wbs[n - 1])
-            if n == B_AT:
-                second_half()
+
+        def ahead(n):
+            if n < len(steps) and n not in rts:
+                if steps[n][0] == 0:
+                    for c in range(steps[n][1] // CH, (steps[n][1] + steps[n][2]) // CH):
+                        damp_first(c)
+                rts[n] = root(*steps[n])
+
+        for n, (g, j0, w) in enumerate(steps):
+            ahead(n)
+            last = j0 + w == HALF
+            if not last or g == 3:
+                ahead(n + 1)
+            rcs[n] = square(rts[n], w, n in SQUARE_ON_VECTOR)
             if g + 1 < 4:
-                damp(g + 1, c)
-            if n + 1 < len(steps) and (c < 3 or g == 3):
-                rcs[n + 1] = square(rts[n + 1], n + 1 in SQUARE_ON_VECTOR)
-            if n + 2 < len(steps) and (c < 2 or g == 3):
-                rts[n + 2] = root(*steps[n + 2])
-            if c == 3 and g < 3:
-                rts[n + 1] = root(*steps[n + 1])
-                rts[n + 2] = root(*steps[n + 2])
-                rcs[n + 1] = square(rts[n + 1], n + 1 in SQUARE_ON_VECTOR)
-            hbs[n] = signal(g, c, rcs[n])
+                for t in range(j0 // CH, (j0 + w) // CH):
+                    damp(g + 1, t)
+            if n == 0 and W11_AT < 0:
+                quant_w1(1, 0, cast_w1(1, 0, W1_ENG[2]))
+                quant_w1(1, 1, cast_w1(1, 1, W1_ENG[3]))
+            hbs[n] = signal(g, j0, w, rcs[n])
             if n >= 1:
-                quant_h(steps[n - 1][0], steps[n - 1][1], hbs[n - 1])
+                quant_h(*steps[n - 1], hbs[n - 1])
+            if n == B_AT - 1:
+                second_half()
+            if n == W11_AT:
+                quant_w1(1, 0, cast_w1(1, 0, W1_ENG[2]))
+                quant_w1(1, 1, cast_w1(1, 1, W1_ENG[3]))
             if g == 2:
-                traits_wide(0, c)
-            if g == 3 and c >= 1:
-                traits_narrow(HALF + (c - 1) * CH)
-        quant_h(3, 3, hbs[15])
-        traits_narrow(HALF + 3 * CH)
+                for nt in range(j0 // CH, (j0 + w) // CH):
+                    traits_wide(0, nt)
+            if g == 3 and j0 > 0:
+                traits_chunk(j0 // CH - 1)
+        quant_h(*steps[-1], hbs[len(steps) - 1])
+        traits_chunk(3)

@@ -19,24 +19,18 @@ ALU = mybir.AluOpType
 P = 128
 PACK = 4
 PASS = P * PACK
-HALF = 512
-CH = 128
-SQUARE_ON_VECTOR = (7,)
-W2_AFTER = (0, 2)
-W1_ENG = ("sv", "vv", "vv", "vv")
-IL_ENG = "ssvvv"
-WIDE_ON_SCALAR = ()
-NARROW = "ssbb"
-WIDTH = (128, 256, 256, 128)
-RES_BUFS = 4
-BB = 4
-XB = 3
-W11_AT = -1
-AB = 2
-RT_BUFS = 3
-RC_BUFS = 6
-B_AT = 0
-HOLD = "picked10"
+QUADS = 4
+PER_COL = 16
+HALF = S // 2
+CHUNK = 128
+LINE = 4
+PAIR = 2
+N_TILES = N // P
+
+EARLY = 256
+STEP_TOKENS = (CHUNK, 2 * CHUNK, 2 * CHUNK, CHUNK)
+B_BANKS, A_BANKS, Y_BANKS = 3, 3, 2
+RECIP_BUFS = 6
 
 
 def tile_list_haplotype_trait_predictor_kernel(
@@ -45,358 +39,329 @@ def tile_list_haplotype_trait_predictor_kernel(
     nc = tc.nc
     with ExitStack() as ctx:
         keep = ctx.enter_context(tc.tile_pool(name="keep", bufs=1))
-        big = ctx.enter_context(tc.tile_pool(name="big", bufs=8))
+        big = ctx.enter_context(tc.tile_pool(name="big", bufs=2 * PACK))
         ring = ctx.enter_context(tc.tile_pool(name="ring", bufs=3))
         psum = ctx.enter_context(tc.psum_pool(name="psum", bufs=1))
 
-        offsets = keep.tile([P, S // 16], U16, name="offsets")
-        wg = [keep.tile([P, HALF], F32, name="wg%d" % half) for half in range(2)]
-        s2raw = keep.tile([P, 2, H], U8, name="s2raw", align_bytes=64)
-        s2 = [keep.tile([P, 2, PASS], U8, name="s2_%d" % b, align_bytes=64) for b in range(2)]
-        w2raw = [keep.tile([P, 2, 2 * PASS], U8, name="w2raw%d" % b, align_bytes=64) for b in range(2)]
-        w2 = [keep.tile([P, 2, 2 * PASS], U8, name="w2_%d" % b, align_bytes=64) for b in range(2)]
+        offsets = keep.tile([P, S // PER_COL], U16, name="offsets")
+        weights = [keep.tile([P, HALF], F32, name="weights%d" % half) for half in range(2)]
+        s2_raw = keep.tile([P, 2, H], U8, name="s2_raw", align_bytes=64)
+        s2 = [keep.tile([P, 2, PASS], U8, name="s2_%d" % blk, align_bytes=64) for blk in range(2)]
+        w2_raw = [keep.tile([P, 2, 2 * PASS], U8, name="w2_raw%d" % blk, align_bytes=64) for blk in range(2)]
+        w2 = [keep.tile([P, 2, 2 * PASS], U8, name="w2_%d" % blk, align_bytes=64) for blk in range(2)]
         w3 = keep.tile([P, 2, N], U32, name="w3", align_bytes=64)
         s3 = keep.tile([P, 2, N], U8, name="s3", align_bytes=64)
-        bias = keep.tile([P, N // P], F32, name="bias")
-        warm = keep.tile([P, 2], F32, name="warm")
+        bias = keep.tile([P, N_TILES], F32, name="bias")
+        unit = keep.tile([P, 3], F32, name="unit")
 
-        nc.gpsimd.memset(s2raw[:].rearrange("p a c -> p (a c)").bitcast(I32), 0)
-        nc.vector.memset(warm[:, 0:1], 1.0)
-        nc.scalar.activation(out=warm[:, 1:2], in_=warm[:, 0:1], func=ACT.Abs_reciprocal_sqrt)
+        nc.gpsimd.memset(s2_raw[:].rearrange("p a c -> p (a c)").bitcast(I32), 0)
+        nc.vector.memset(unit[:, 0:1], 1.0)
+        nc.scalar.activation(out=unit[:, 1:2], in_=unit[:, 0:1], func=ACT.Abs_reciprocal_sqrt)
+        nc.scalar.activation(out=unit[:, 2:3], in_=unit[:, 1:2], func=ACT.Sign)
+        one = unit[:, 2:3]
         nc.vector.memset(s3[:].rearrange("p a c -> p (a c)").bitcast(I32), 0)
 
-        nc.sync.dma_start(offsets[:], offs)
-
-        def load_s2():
-            for q in range(4):
+        def load_scales(tile, scales):
+            for quad in range(QUADS):
                 nc.sync.dma_start(
-                    out=s2raw[32 * q : 32 * q + 4, :, :].bitcast(I32),
-                    in_=w2_scales.bitcast(I32)[:, 4 * q : 4 * q + 4, :].rearrange("a r c -> r a c"),
+                    out=tile[32 * quad : 32 * quad + 4, :, :].bitcast(I32),
+                    in_=scales.bitcast(I32)[:, 4 * quad : 4 * quad + 4, :].rearrange("a r c -> r a c"),
                 )
 
         def load_w2(blk):
-            cols = slice(blk * PASS // 2, (blk + 1) * PASS // 2)
+            words = slice(blk * PASS // 2, (blk + 1) * PASS // 2)
             nc.sync.dma_start(
-                out=w2raw[blk][:].bitcast(I32),
-                in_=w2_words.bitcast(I32)[:, :, cols].rearrange("a p c -> p a c"),
+                out=w2_raw[blk][:].bitcast(I32),
+                in_=w2_words.bitcast(I32)[:, :, words].rearrange("a p c -> p a c"),
             )
 
-        nc.sync.dma_start(out=wg[0][:], in_=wgt[:, 0:HALF])
-        load_s2()
-        planes = []
-        w1raw = {}
+        w1_raw = {}
 
         def load_w1(blk, a):
-            raw = keep.tile([P, PACK, PASS], F32, name="w1raw", tag="w1raw%d%d" % (blk, a))
+            w1_raw[blk, a] = keep.tile([P, PACK, PASS], F32, name="w1_raw%d%d" % (blk, a))
             nc.sync.dma_start(
-                out=raw[:],
+                out=w1_raw[blk, a][:],
                 in_=w1[a * PASS : (a + 1) * PASS, blk * PASS : (blk + 1) * PASS].rearrange(
                     "(p i) c -> p i c", i=PACK
                 ),
             )
-            w1raw[blk, a] = raw
 
-        for a in range(2):
+        planes = {}
+
+        def load_plane(a, i):
+            planes[a, i] = big.tile([P, T], F32, name="plane", tag="big")
             rows = xT[a * PASS : (a + 1) * PASS, :].rearrange("(p i) t -> p i t", i=PACK)
-            for i in range(PACK):
-                plane = big.tile([P, T], F32, name="plane", tag="big")
-                nc.sync.dma_start(out=plane[:], in_=rows[:, i, :])
-                planes.append(plane)
-                if (a, i) == (0, 0):
-                    nc.sync.dma_start(out=wg[1][:], in_=wgt[:, HALF:S])
-                if (a, i) == W2_AFTER:
-                    load_w2(0)
+            nc.sync.dma_start(out=planes[a, i][:], in_=rows[:, i, :])
+
+        nc.sync.dma_start(offsets[:], offs)
+        nc.sync.dma_start(out=weights[0][:], in_=wgt[:, 0:HALF])
+        load_scales(s2_raw, w2_scales)
+        load_plane(0, 0)
+        nc.sync.dma_start(out=weights[1][:], in_=wgt[:, HALF:S])
+        for i in range(1, PACK - 1):
+            load_plane(0, i)
+        load_w2(0)
+        load_plane(0, PACK - 1)
+        for i in range(PACK):
+            load_plane(1, i)
         load_w1(0, 0)
         load_w2(1)
         load_w1(0, 1)
         load_w1(1, 0)
         load_w1(1, 1)
-        nc.sync.dma_start(
-            out=w3[:].bitcast(I32), in_=w3_words.rearrange("a p n t -> p a (n t)").bitcast(I32)
-        )
-        for q in range(4):
-            nc.sync.dma_start(
-                out=s3[32 * q : 32 * q + 4, :, :].bitcast(I32),
-                in_=w3_scales.bitcast(I32)[:, 4 * q : 4 * q + 4, :].rearrange("a r c -> r a c"),
-            )
-        with nc.allow_non_contiguous_dma(reason="one bias value a partition"):
+        nc.sync.dma_start(out=w3[:].bitcast(I32), in_=w3_words.rearrange("a p n t -> p a (n t)").bitcast(I32))
+        load_scales(s3, w3_scales)
+        with nc.allow_non_contiguous_dma(reason="output row 128 c + p takes its bias on partition p"):
             nc.sync.dma_start(out=bias[:], in_=bt.rearrange("(c p) -> p c", p=P))
+
+        def quantise(woven, codes, scales):
+            nc.vector.quantize_mx(
+                out=codes.bitcast(FP8X4), scales=scales, in_=woven[:].rearrange("p c i -> p (c i)")
+            )
 
         def deal_w2(blk):
             nc.vector.tensor_copy(
                 out=w2[blk][:].bitcast(U16).rearrange("p a (t m) -> p a t m", t=PACK),
-                in_=w2raw[blk][:].bitcast(U16).rearrange("p a (m t) -> p a t m", t=PACK),
+                in_=w2_raw[blk][:].bitcast(U16).rearrange("p a (m t) -> p a t m", t=PACK),
             )
 
         def deal_s2(blk):
             nc.vector.tensor_copy(
                 out=s2[blk][:].rearrange("p a (t m) -> p a t m", t=PACK),
-                in_=s2raw[:, :, blk * PASS : (blk + 1) * PASS].rearrange("p a (m t) -> p a t m", t=PACK),
+                in_=s2_raw[:, :, blk * PASS : (blk + 1) * PASS].rearrange("p a (m t) -> p a t m", t=PACK),
             )
 
         xq = [keep.tile([P, S], U32, name="xq%d" % a, align_bytes=64) for a in range(2)]
         xs = [keep.tile([P, S], U8, name="xs%d" % a, align_bytes=64) for a in range(2)]
-        picked = {}
 
-        def gather(a, i, half, j0=0, n=HALF):
-            if (a, half) not in picked:
-                tag = HOLD if (a, half) == (1, 1) else "picked%d%d" % (a, half)
-                picked[a, half] = keep.tile([P, PACK, HALF], F32, name="picked", tag=tag)
-            j = half * HALF + j0
+        def picks_tile(width, tag):
+            return keep.tile([P, PACK, width], F32, name="picks", tag=tag)
+
+        def gather(picks, c0, a, i, j0, n):
             nc.vector.tensor_tensor(
-                picked[a, half][:, i, j0 : j0 + n],
-                planes[PACK * a + i][:].indirect(offsets[:, j // 16 : (j + n) // 16]),
-                wg[half][:, j0 : j0 + n],
+                picks[:, i, c0 : c0 + n],
+                planes[a, i][:].indirect(offsets[:, j0 // PER_COL : (j0 + n) // PER_COL]),
+                weights[j0 // HALF][:, j0 % HALF : j0 % HALF + n],
                 ALU.mult,
             )
 
-        def weave_x(a, half, j0, n, eng="s"):
-            xb = ring.tile([P, n, PACK], BF16, name="xb", tag="xb", bufs=XB, align_bytes=64)
-            (nc.scalar.copy if eng == "s" else nc.vector.tensor_copy)(
-                out=xb[:].rearrange("p (c e) i -> p c i e", e=2),
-                in_=picked[a, half][:, :, j0 : j0 + n].rearrange("p i (c e) -> p c i e", e=2),
+        def weave_x(copy, picks, c0, n):
+            xb = ring.tile([P, n, PACK], BF16, name="xb", align_bytes=64)
+            copy(
+                out=xb[:].rearrange("p (c e) i -> p c i e", e=LINE),
+                in_=picks[:, :, c0 : c0 + n].rearrange("p i (c e) -> p c i e", e=LINE),
             )
             return xb
 
-        def quant_x(a, half, j0, n, xb):
-            j = half * HALF + j0
-            quant(xb, xq[a][:, j : j + n], xs[a][:, j : j + n])
-
-        def quant(src, codes, scales):
-            nc.vector.quantize_mx(
-                out=codes.bitcast(FP8X4), scales=scales, in_=src[:].rearrange("p c i -> p (c i)")
-            )
+        def quantise_x(xb, a, j0, n):
+            quantise(xb, xq[a][:, j0 : j0 + n], xs[a][:, j0 : j0 + n])
 
         w1q = {}
         w1s = {}
 
-        def cast_w1(blk, a, eng):
-            wb = ring.tile([P, PASS, PACK], BF16, name="wb", tag="wb", bufs=2, align_bytes=64)
-            for u in range(2):
-                dst = wb[:].rearrange("p (u e m) i -> p u m i e", u=2, e=2)[:, u]
-                src = w1raw[blk, a][:].rearrange("p i (m u e) -> p u m i e", u=2, e=2)[:, u]
-                if eng[u] == "s":
-                    nc.scalar.copy(out=dst, in_=src)
-                else:
-                    nc.vector.tensor_copy(out=dst, in_=src)
-            return wb
-
-        def quant_w1(blk, a, wb):
+        def quantise_w1(blk, a):
+            wb = ring.tile([P, PASS, PACK], BF16, name="wb", bufs=2, align_bytes=64)
+            for u in range(PACK // PAIR):
+                nc.vector.tensor_copy(
+                    out=wb[:].rearrange("p (u e m) i -> p u m i e", u=PACK // PAIR, e=PAIR)[:, u],
+                    in_=w1_raw[blk, a][:].rearrange("p i (m u e) -> p u m i e", u=PACK // PAIR, e=PAIR)[:, u],
+                )
             w1q[blk, a] = keep.tile([P, PASS], U32, name="w1q%d%d" % (blk, a), align_bytes=64)
             w1s[blk, a] = keep.tile([P, PASS], U8, name="w1s%d%d" % (blk, a), align_bytes=64)
-            quant(wb, w1q[blk, a][:], w1s[blk, a][:])
+            quantise(wb, w1q[blk, a][:], w1s[blk, a][:])
 
-        deal_s2(0)
-        deal_s2(1)
+        for blk in range(2):
+            deal_s2(blk)
+        picks0 = [picks_tile(HALF, "spare%d" % half) for half in range(2)]
         for i in range(PACK):
-            gather(0, i, 0)
-            gather(0, i, 1)
-        xb00 = weave_x(0, 0, 0, HALF)
-        xb01 = weave_x(0, 1, 0, HALF)
+            for half in range(2):
+                gather(picks0[half], 0, 0, i, half * HALF, HALF)
+        xb0 = [weave_x(nc.scalar.copy, picks0[half], 0, HALF) for half in range(2)]
+        picks1 = picks_tile(HALF, "picks1")
         for i in range(PACK - 1):
-            gather(1, i, 0)
-        quant_x(0, 0, 0, HALF, xb00)
+            gather(picks1, 0, 1, i, 0, HALF)
+        quantise_x(xb0[0], 0, 0, HALF)
         deal_w2(0)
-        for c in range(4):
-            gather(1, PACK - 1, 0, c * CH, CH)
-            quant_x(1, 0, c * CH, CH, weave_x(1, 0, c * CH, CH, IL_ENG[c]))
+        for j0 in range(0, HALF, CHUNK):
+            gather(picks1, j0, 1, PACK - 1, j0, CHUNK)
+            quantise_x(weave_x(nc.scalar.copy, picks1, j0, CHUNK), 1, j0, CHUNK)
         deal_w2(1)
-
-        def second_half():
+        for a in range(2):
+            quantise_w1(0, a)
+        for j0, n, tag in ((HALF, EARLY, "early"), (HALF + EARLY, HALF - EARLY, "picks1")):
+            picks = picks_tile(n, tag)
             for i in range(PACK):
-                gather(1, i, 1)
-            quant_x(1, 1, 0, HALF, weave_x(1, 1, 0, HALF, IL_ENG[4]))
+                gather(picks, 0, 1, i, j0, n)
+            quantise_x(weave_x(nc.vector.tensor_copy, picks, 0, n), 1, j0, n)
+        quantise_x(xb0[1], 0, HALF, HALF)
 
-        if B_AT == -2:
-            second_half()
-        quant_w1(0, 0, cast_w1(0, 0, W1_ENG[0]))
-        if B_AT == -1:
-            second_half()
-        quant_w1(0, 1, cast_w1(0, 1, W1_ENG[1]))
-        if B_AT == 0:
-            second_half()
-        quant_x(0, 1, 0, HALF, xb01)
-
-        hq = [keep.tile([P, S], U32, name="hq%d" % b, align_bytes=64) for b in range(2)]
-        hs = [keep.tile([P, S], U8, name="hs%d" % b, align_bytes=64) for b in range(2)]
+        hq = [keep.tile([P, S], U32, name="hq%d" % blk, align_bytes=64) for blk in range(2)]
+        hs = [keep.tile([P, S], U8, name="hs%d" % blk, align_bytes=64) for blk in range(2)]
         groups = [(blk, half) for half in range(2) for blk in range(2)]
+        last_group = len(groups) - 1
         mags = {}
 
-        def damp(g, t):
-            blk, half = groups[g]
-            if t == 0:
-                mags[g] = keep.tile([P, PACK, HALF], F32, name="mag", tag="picked00")
-            cols = slice(half * HALF, (half + 1) * HALF)
-            bank = psum.tile([P, HALF], F32, name="bbank", tag="bbank", bufs=BB)
-            c0 = t * P
-            for a in range(2):
-                nc.tensor.matmul_mx(
-                    out=bank[:],
-                    lhsT=w2[blk][:, a, 2 * c0 : 2 * (c0 + P)].bitcast(FP4X4),
-                    lhsT_scale=s2[blk][:, a, c0 : c0 + P],
-                    rhs=xq[a][:, cols].bitcast(FP8X4),
-                    rhs_scale=xs[a][:, cols],
-                    start=(a == 0),
-                    stop=(a == 1),
-                )
-            nc.scalar.activation(out=mags[g][:, t, :], in_=bank[:], func=ACT.Abs)
+        def b_pass(bank, blk, a, t, cols, start, stop):
+            nc.tensor.matmul_mx(
+                out=bank,
+                lhsT=w2[blk][:, a, 2 * t * P : 2 * (t + 1) * P].bitcast(FP4X4),
+                lhsT_scale=s2[blk][:, a, t * P : (t + 1) * P],
+                rhs=xq[a][:, cols].bitcast(FP8X4),
+                rhs_scale=xs[a][:, cols],
+                start=start,
+                stop=stop,
+            )
 
-        def damp_first(c):
-            if c == 0:
-                mags[0] = keep.tile([P, PACK, HALF], F32, name="mag", tag="picked00")
-            cols = slice(c * CH, (c + 1) * CH)
-            bank = psum.tile([P, PACK, CH], F32, name="bbank", tag="bbank", bufs=BB)
+        def damping_chunk(j0):
+            if j0 == 0:
+                mags[0] = keep.tile([P, HALF, PACK], F32, name="mag", tag="spare0")
+            bank = psum.tile([P, PACK, CHUNK], F32, name="b_bank", bufs=B_BANKS)
             for a in range(2):
                 for t in range(PACK):
-                    nc.tensor.matmul_mx(
-                        out=bank[:, t, :],
-                        lhsT=w2[0][:, a, 2 * t * P : 2 * (t + 1) * P].bitcast(FP4X4),
-                        lhsT_scale=s2[0][:, a, t * P : (t + 1) * P],
-                        rhs=xq[a][:, cols].bitcast(FP8X4),
-                        rhs_scale=xs[a][:, cols],
-                        start=(a == 0 and t == 0),
-                        stop=(a == 1 and t == PACK - 1),
-                    )
-            nc.scalar.activation(out=mags[0][:, :, cols], in_=bank[:], func=ACT.Abs)
-
-        def root(g, j0, n):
-            rt = ring.tile([P, PACK, n], F32, name="rt", tag="rt", bufs=RT_BUFS)
+                    first, final = (a, t) == (0, 0), (a, t) == (1, PACK - 1)
+                    b_pass(bank[:, t, :], 0, a, t, slice(j0, j0 + CHUNK), first, final)
             nc.scalar.activation(
-                out=rt[:], in_=mags[g][:, :, j0 : j0 + n], func=ACT.Abs_reciprocal_sqrt, bias=1.0
+                out=mags[0][:, j0 : j0 + CHUNK, :], in_=bank[:].rearrange("p t n -> p n t"), func=ACT.Abs
             )
-            return rt
 
-        def square(rt, n, on_vector):
-            rc = ring.tile([P, PACK, n], F32, name="rc", tag="rc", bufs=RC_BUFS)
-            if on_vector:
-                nc.vector.tensor_tensor(rc[:], rt[:], rt[:], ALU.mult)
-            else:
-                nc.scalar.activation(out=rc[:], in_=rt[:], func=ACT.Square)
-            return rc
-
-        def signal(g, j0, n, rc):
+        def damping_wide(g, t):
             blk, half = groups[g]
-            hb = ring.tile([P, n, PACK], BF16, name="hb", tag="hb", align_bytes=64)
-            for c0 in range(0, n, CH):
-                j = half * HALF + j0 + c0
-                bank = psum.tile([P, PACK, CH], F32, name="abank", tag="abank", bufs=AB)
+            if t == 0:
+                mags[g] = keep.tile([P, PACK, HALF], F32, name="mag", tag="spare%d" % (g % 2))
+            bank = psum.tile([P, HALF], F32, name="b_bank", bufs=B_BANKS)
+            for a in range(2):
+                b_pass(bank[:], blk, a, t, slice(half * HALF, (half + 1) * HALF), a == 0, a == 1)
+            nc.scalar.activation(out=mags[g][:, t, :], in_=bank[:], func=ACT.Abs)
+
+        def inverse_root(g, j0, n):
+            root = ring.tile([P, n, PACK], F32, name="root")
+            if g == 0:
+                dst = root[:].rearrange("p n t -> p (n t)")
+                src = mags[0][:, j0 : j0 + n, :].rearrange("p n t -> p (n t)")
+            else:
+                dst = root[:].rearrange("p (c e) t -> p c t e", e=PAIR)
+                src = mags[g][:, :, j0 : j0 + n].rearrange("p t (c e) -> p c t e", e=PAIR)
+            nc.scalar.activation(out=dst, in_=src, func=ACT.Abs_reciprocal_sqrt, bias=one)
+            return root
+
+        def reciprocal(root, g, j0, n):
+            recip = ring.tile([P, n, PACK], F32, name="recip", bufs=RECIP_BUFS)
+            if 0 < g < last_group and j0 + n == HALF:
+                nc.vector.tensor_tensor(recip[:], root[:], root[:], ALU.mult)
+            else:
+                nc.scalar.activation(out=recip[:], in_=root[:], func=ACT.Square)
+            return recip
+
+        def signal(recip, g, j0, n):
+            blk, half = groups[g]
+            hb = ring.tile([P, n, PACK], BF16, name="hb", align_bytes=64)
+            for c0 in range(0, n, CHUNK):
+                cols = slice(half * HALF + j0 + c0, half * HALF + j0 + c0 + CHUNK)
+                bank = psum.tile([P, PACK, CHUNK], F32, name="a_bank", bufs=A_BANKS)
                 for t in range(PACK):
                     for a in range(2):
                         nc.tensor.matmul_mx(
                             out=bank[:, t, :],
                             lhsT=w1q[blk, a][:, t * P : (t + 1) * P].bitcast(FP8X4),
                             lhsT_scale=w1s[blk, a][:, t * P : (t + 1) * P],
-                            rhs=xq[a][:, j : j + CH].bitcast(FP8X4),
-                            rhs_scale=xs[a][:, j : j + CH],
+                            rhs=xq[a][:, cols].bitcast(FP8X4),
+                            rhs_scale=xs[a][:, cols],
                             start=(a == 0),
                             stop=(a == 1),
                         )
                 nc.vector.tensor_tensor(
-                    hb[:, c0 : c0 + CH, :].rearrange("p (c e) t -> p c t e", e=2),
-                    bank[:].rearrange("p t (c e) -> p c t e", e=2),
-                    rc[:, :, c0 : c0 + CH].rearrange("p t (c e) -> p c t e", e=2),
+                    hb[:, c0 : c0 + CHUNK, :],
+                    bank[:].rearrange("p t n -> p n t"),
+                    recip[:, c0 : c0 + CHUNK, :],
                     ALU.mult,
                 )
             return hb
 
-        def quant_h(g, j0, n, hb):
+        def quantise_h(hb, g, j0, n):
             blk, half = groups[g]
-            j = half * HALF + j0
-            quant(hb, hq[blk][:, j : j + n], hs[blk][:, j : j + n])
+            cols = slice(half * HALF + j0, half * HALF + j0 + n)
+            quantise(hb, hq[blk][:, cols], hs[blk][:, cols])
 
-        def traits_wide(j0, nt):
-            bank = psum.tile([P, HALF], F32, name="ybank", tag="ybank", bufs=2)
-            for b in range(2):
-                nc.tensor.matmul_mx(
-                    out=bank[:],
-                    lhsT=w3[:, b, nt * P : (nt + 1) * P].bitcast(FP8X4),
-                    lhsT_scale=s3[:, b, nt * P : (nt + 1) * P],
-                    rhs=hq[b][:, j0 : j0 + HALF].bitcast(FP8X4),
-                    rhs_scale=hs[b][:, j0 : j0 + HALF],
-                    start=(b == 0),
-                    stop=(b == 1),
-                )
+        def y_pass(bank, blk, nt, cols, start, stop):
+            nc.tensor.matmul_mx(
+                out=bank,
+                lhsT=w3[:, blk, nt * P : (nt + 1) * P].bitcast(FP8X4),
+                lhsT_scale=s3[:, blk, nt * P : (nt + 1) * P],
+                rhs=hq[blk][:, cols].bitcast(FP8X4),
+                rhs_scale=hs[blk][:, cols],
+                start=start,
+                stop=stop,
+            )
+
+        def traits_wide(nt):
+            bank = psum.tile([P, HALF], F32, name="y_bank", bufs=Y_BANKS)
+            for blk in range(2):
+                y_pass(bank[:], blk, nt, slice(0, HALF), blk == 0, blk == 1)
             res = big.tile([P, HALF], F32, name="res", tag="big")
-            if nt in WIDE_ON_SCALAR:
-                nc.scalar.activation(out=res[:], in_=bank[:], func=ACT.Identity, bias=bias[:, nt : nt + 1])
-            else:
-                nc.vector.tensor_scalar(
-                    out=res[:], in0=bank[:], scalar1=bias[:, nt : nt + 1], scalar2=None, op0=ALU.add
-                )
-            nc.sync.dma_start(out=out[nt * P : (nt + 1) * P, j0 : j0 + HALF], in_=res[:])
+            nc.vector.tensor_scalar(out=res[:], in0=bank[:], scalar1=bias[:, nt : nt + 1], scalar2=None, op0=ALU.add)
+            nc.sync.dma_start(out=out[nt * P : (nt + 1) * P, 0:HALF], in_=res[:])
 
-        def traits_narrow(j0, nt0, count, tag, bufs, on_scalar):
-            bank = psum.tile([P, count, CH], F32, name="ybank", tag=tag, bufs=bufs)
-            for b in range(2):
+        def traits_rows(bank, j0, nt0, count, on_scalar):
+            cols = slice(j0, j0 + CHUNK)
+            for blk in range(2):
                 for k in range(count):
-                    nt = nt0 + k
-                    nc.tensor.matmul_mx(
-                        out=bank[:, k, :],
-                        lhsT=w3[:, b, nt * P : (nt + 1) * P].bitcast(FP8X4),
-                        lhsT_scale=s3[:, b, nt * P : (nt + 1) * P],
-                        rhs=hq[b][:, j0 : j0 + CH].bitcast(FP8X4),
-                        rhs_scale=hs[b][:, j0 : j0 + CH],
-                        start=(b == 0 and k == 0),
-                        stop=(b == 1 and k == count - 1),
-                    )
-            res = big.tile([P, count, CH], F32, name="res", tag="big")
+                    y_pass(bank[:, k, :], blk, nt0 + k, cols, (blk, k) == (0, 0), (blk, k) == (1, count - 1))
+            res = big.tile([P, count, CHUNK], F32, name="res", tag="big")
             if on_scalar:
                 for k in range(count):
                     nc.scalar.activation(
                         out=res[:, k, :], in_=bank[:, k, :], func=ACT.Identity, bias=bias[:, nt0 + k : nt0 + k + 1]
                     )
             else:
-                nc.vector.tensor_tensor(
-                    res[:], bank[:], bias[:, nt0 : nt0 + count].unsqueeze(2).to_broadcast([P, count, CH]), ALU.add
-                )
-            (nc.scalar if on_scalar else nc.sync).dma_start(
-                out=out[nt0 * P : (nt0 + count) * P, j0 : j0 + CH].rearrange("(c p) j -> p c j", p=P), in_=res[:]
+                rows_bias = bias[:, nt0 : nt0 + count].unsqueeze(2).to_broadcast([P, count, CHUNK])
+                nc.vector.tensor_tensor(res[:], bank[:], rows_bias, ALU.add)
+            nc.sync.dma_start(
+                out=out[nt0 * P : (nt0 + count) * P, cols].rearrange("(c p) j -> p c j", p=P), in_=res[:]
             )
 
-        def traits_chunk(c):
-            j0 = HALF + c * CH
-            if NARROW[c] == "b":
-                traits_narrow(j0, 0, 2, "ybank", 2, False)
-                traits_narrow(j0, 2, 2, "bbank", BB, True)
+        def traits_chunk(j0):
+            if j0 == HALF:
+                bank = psum.tile([P, N_TILES, CHUNK], F32, name="y_bank", bufs=Y_BANKS)
+                traits_rows(bank, j0, 0, N_TILES, True)
             else:
-                traits_narrow(j0, 0, 4, "ybank", 2, NARROW[c] == "s")
+                count = N_TILES // 2
+                bank = psum.tile([P, count, CHUNK], F32, name="y_bank", bufs=Y_BANKS)
+                traits_rows(bank, j0, 0, count, False)
+                bank = psum.tile([P, count, CHUNK], F32, name="b_bank", bufs=B_BANKS)
+                traits_rows(bank, j0, count, count, True)
 
-        steps = [(g, j0, WIDTH[g]) for g in range(4) for j0 in range(0, HALF, WIDTH[g])]
-        rts = {}
-        rcs = {}
-        hbs = {}
+        steps = [(g, j0, n) for g, n in enumerate(STEP_TOKENS) for j0 in range(0, HALF, n)]
+        roots = {}
 
-        def ahead(n):
-            if n < len(steps) and n not in rts:
-                if steps[n][0] == 0:
-                    for c in range(steps[n][1] // CH, (steps[n][1] + steps[n][2]) // CH):
-                        damp_first(c)
-                rts[n] = root(*steps[n])
+        def make_root(step):
+            g, j0, n = step
+            if step not in roots:
+                if g == 0:
+                    damping_chunk(j0)
+                roots[step] = inverse_root(g, j0, n)
 
-        for n, (g, j0, w) in enumerate(steps):
-            ahead(n)
-            last = j0 + w == HALF
-            if not last or g == 3:
-                ahead(n + 1)
-            rcs[n] = square(rts[n], w, n in SQUARE_ON_VECTOR)
-            if g + 1 < 4:
-                for t in range(j0 // CH, (j0 + w) // CH):
-                    damp(g + 1, t)
-            if n == 0 and W11_AT < 0:
-                quant_w1(1, 0, cast_w1(1, 0, W1_ENG[2]))
-                quant_w1(1, 1, cast_w1(1, 1, W1_ENG[3]))
-            hbs[n] = signal(g, j0, w, rcs[n])
-            if n >= 1:
-                quant_h(*steps[n - 1], hbs[n - 1])
-            if n == B_AT - 1:
-                second_half()
-            if n == W11_AT:
-                quant_w1(1, 0, cast_w1(1, 0, W1_ENG[2]))
-                quant_w1(1, 1, cast_w1(1, 1, W1_ENG[3]))
-            if g == 2:
-                for nt in range(j0 // CH, (j0 + w) // CH):
-                    traits_wide(0, nt)
-            if g == 3 and j0 > 0:
-                traits_chunk(j0 // CH - 1)
-        quant_h(*steps[-1], hbs[len(steps) - 1])
-        traits_chunk(3)
+        before = None
+        for step in steps:
+            g, j0, n = step
+            share = range(j0 // CHUNK, (j0 + n) // CHUNK)
+            make_root(step)
+            if j0 + n < HALF:
+                make_root((g, j0 + n, n))
+            recip = reciprocal(roots[step], g, j0, n)
+            if g < last_group:
+                for t in share:
+                    damping_wide(g + 1, t)
+            if before is None:
+                for a in range(2):
+                    quantise_w1(1, a)
+            hb = signal(recip, g, j0, n)
+            if before is not None:
+                quantise_h(*before)
+            before = (hb, g, j0, n)
+            if g == last_group - 1:
+                for nt in share:
+                    traits_wide(nt)
+            if g == last_group and j0 > 0:
+                traits_chunk(HALF + j0 - CHUNK)
+        quantise_h(*before)
+        traits_chunk(S - CHUNK)

from contextlib import ExitStack

import concourse.mybir as mybir

K, T, S, H, N = 1024, 2048, 1024, 1024, 512
FLOPS = 2 * (2 * K * H * S + H * N * S)

F32 = mybir.dt.float32
BF16 = mybir.dt.bfloat16
I32 = mybir.dt.int32
U32 = mybir.dt.uint32
U16 = mybir.dt.uint16
U8 = mybir.dt.uint8
FP8X4 = mybir.dt.float8_e4m3fn_x4
FP4X4 = mybir.dt.float4_e2m1fn_x4
ACT = mybir.ActivationFunctionType
ALU = mybir.AluOpType

P = 128
PACK = 4
PASS = P * PACK
QUADS = 4
PER_COL = 16
HALF = S // 2
CHUNK = 128
LINE = 4
PAIR = 2
N_TILES = N // P

EARLY = 256
STEP_TOKENS = (CHUNK, 2 * CHUNK, 2 * CHUNK, CHUNK)
B_BANKS, A_BANKS, Y_BANKS = 3, 3, 2
RECIP_BUFS = 6


def tile_list_haplotype_trait_predictor_kernel(
    tc, xT, wgt, offs, w1, w2_words, w2_scales, w3_words, w3_scales, bt, out
):
    nc = tc.nc
    with ExitStack() as ctx:
        keep = ctx.enter_context(tc.tile_pool(name="keep", bufs=1))
        big = ctx.enter_context(tc.tile_pool(name="big", bufs=2 * PACK))
        ring = ctx.enter_context(tc.tile_pool(name="ring", bufs=3))
        psum = ctx.enter_context(tc.psum_pool(name="psum", bufs=1))

        offsets = keep.tile([P, S // PER_COL], U16, name="offsets")
        weights = [keep.tile([P, HALF], F32, name="weights%d" % half) for half in range(2)]
        s2_raw = keep.tile([P, 2, H], U8, name="s2_raw", align_bytes=64)
        s2 = [keep.tile([P, 2, PASS], U8, name="s2_%d" % blk, align_bytes=64) for blk in range(2)]
        w2_raw = [keep.tile([P, 2, 2 * PASS], U8, name="w2_raw%d" % blk, align_bytes=64) for blk in range(2)]
        w2 = [keep.tile([P, 2, 2 * PASS], U8, name="w2_%d" % blk, align_bytes=64) for blk in range(2)]
        w3 = keep.tile([P, 2, N], U32, name="w3", align_bytes=64)
        s3 = keep.tile([P, 2, N], U8, name="s3", align_bytes=64)
        bias = keep.tile([P, N_TILES], F32, name="bias")
        unit = keep.tile([P, 3], F32, name="unit")

        nc.gpsimd.memset(s2_raw[:].rearrange("p a c -> p (a c)").bitcast(I32), 0)
        nc.vector.memset(unit[:, 0:1], 1.0)
        nc.scalar.activation(out=unit[:, 1:2], in_=unit[:, 0:1], func=ACT.Abs_reciprocal_sqrt)
        nc.scalar.activation(out=unit[:, 2:3], in_=unit[:, 1:2], func=ACT.Sign)
        one = unit[:, 2:3]
        nc.vector.memset(s3[:].rearrange("p a c -> p (a c)").bitcast(I32), 0)

        def load_scales(tile, scales):
            for quad in range(QUADS):
                nc.sync.dma_start(
                    out=tile[32 * quad : 32 * quad + 4, :, :].bitcast(I32),
                    in_=scales.bitcast(I32)[:, 4 * quad : 4 * quad + 4, :].rearrange("a r c -> r a c"),
                )

        def load_w2(blk):
            words = slice(blk * PASS // 2, (blk + 1) * PASS // 2)
            nc.sync.dma_start(
                out=w2_raw[blk][:].bitcast(I32),
                in_=w2_words.bitcast(I32)[:, :, words].rearrange("a p c -> p a c"),
            )

        w1_raw = {}

        def load_w1(blk, a):
            w1_raw[blk, a] = keep.tile([P, PACK, PASS], F32, name="w1_raw%d%d" % (blk, a))
            nc.sync.dma_start(
                out=w1_raw[blk, a][:],
                in_=w1[a * PASS : (a + 1) * PASS, blk * PASS : (blk + 1) * PASS].rearrange(
                    "(p i) c -> p i c", i=PACK
                ),
            )

        planes = {}

        def load_plane(a, i):
            planes[a, i] = big.tile([P, T], F32, name="plane", tag="big")
            rows = xT[a * PASS : (a + 1) * PASS, :].rearrange("(p i) t -> p i t", i=PACK)
            nc.sync.dma_start(out=planes[a, i][:], in_=rows[:, i, :])

        nc.sync.dma_start(offsets[:], offs)
        nc.sync.dma_start(out=weights[0][:], in_=wgt[:, 0:HALF])
        load_scales(s2_raw, w2_scales)
        load_plane(0, 0)
        nc.sync.dma_start(out=weights[1][:], in_=wgt[:, HALF:S])
        for i in range(1, PACK - 1):
            load_plane(0, i)
        load_w2(0)
        load_plane(0, PACK - 1)
        for i in range(PACK):
            load_plane(1, i)
        load_w1(0, 0)
        load_w2(1)
        load_w1(0, 1)
        load_w1(1, 0)
        load_w1(1, 1)
        nc.sync.dma_start(out=w3[:].bitcast(I32), in_=w3_words.rearrange("a p n t -> p a (n t)").bitcast(I32))
        load_scales(s3, w3_scales)
        with nc.allow_non_contiguous_dma(reason="output row 128 c + p takes its bias on partition p"):
            nc.sync.dma_start(out=bias[:], in_=bt.rearrange("(c p) -> p c", p=P))

        def quantise(woven, codes, scales):
            nc.vector.quantize_mx(
                out=codes.bitcast(FP8X4), scales=scales, in_=woven[:].rearrange("p c i -> p (c i)")
            )

        def deal_w2(blk):
            nc.vector.tensor_copy(
                out=w2[blk][:].bitcast(U16).rearrange("p a (t m) -> p a t m", t=PACK),
                in_=w2_raw[blk][:].bitcast(U16).rearrange("p a (m t) -> p a t m", t=PACK),
            )

        def deal_s2(blk):
            nc.vector.tensor_copy(
                out=s2[blk][:].rearrange("p a (t m) -> p a t m", t=PACK),
                in_=s2_raw[:, :, blk * PASS : (blk + 1) * PASS].rearrange("p a (m t) -> p a t m", t=PACK),
            )

        xq = [keep.tile([P, S], U32, name="xq%d" % a, align_bytes=64) for a in range(2)]
        xs = [keep.tile([P, S], U8, name="xs%d" % a, align_bytes=64) for a in range(2)]

        def picks_tile(width, tag):
            return keep.tile([P, PACK, width], F32, name="picks", tag=tag)

        def gather(picks, c0, a, i, j0, n):
            nc.vector.tensor_tensor(
                picks[:, i, c0 : c0 + n],
                planes[a, i][:].indirect(offsets[:, j0 // PER_COL : (j0 + n) // PER_COL]),
                weights[j0 // HALF][:, j0 % HALF : j0 % HALF + n],
                ALU.mult,
            )

        def weave_x(copy, picks, c0, n):
            xb = ring.tile([P, n, PACK], BF16, name="xb", align_bytes=64)
            copy(
                out=xb[:].rearrange("p (c e) i -> p c i e", e=LINE),
                in_=picks[:, :, c0 : c0 + n].rearrange("p i (c e) -> p c i e", e=LINE),
            )
            return xb

        def quantise_x(xb, a, j0, n):
            quantise(xb, xq[a][:, j0 : j0 + n], xs[a][:, j0 : j0 + n])

        w1q = {}
        w1s = {}

        def quantise_w1(blk, a):
            wb = ring.tile([P, PASS, PACK], BF16, name="wb", bufs=2, align_bytes=64)
            for u in range(PACK // PAIR):
                nc.vector.tensor_copy(
                    out=wb[:].rearrange("p (u e m) i -> p u m i e", u=PACK // PAIR, e=PAIR)[:, u],
                    in_=w1_raw[blk, a][:].rearrange("p i (m u e) -> p u m i e", u=PACK // PAIR, e=PAIR)[:, u],
                )
            w1q[blk, a] = keep.tile([P, PASS], U32, name="w1q%d%d" % (blk, a), align_bytes=64)
            w1s[blk, a] = keep.tile([P, PASS], U8, name="w1s%d%d" % (blk, a), align_bytes=64)
            quantise(wb, w1q[blk, a][:], w1s[blk, a][:])

        for blk in range(2):
            deal_s2(blk)
        picks0 = [picks_tile(HALF, "spare%d" % half) for half in range(2)]
        for i in range(PACK):
            for half in range(2):
                gather(picks0[half], 0, 0, i, half * HALF, HALF)
        xb0 = [weave_x(nc.scalar.copy, picks0[half], 0, HALF) for half in range(2)]
        picks1 = picks_tile(HALF, "picks1")
        for i in range(PACK - 1):
            gather(picks1, 0, 1, i, 0, HALF)
        quantise_x(xb0[0], 0, 0, HALF)
        deal_w2(0)
        for j0 in range(0, HALF, CHUNK):
            gather(picks1, j0, 1, PACK - 1, j0, CHUNK)
            quantise_x(weave_x(nc.scalar.copy, picks1, j0, CHUNK), 1, j0, CHUNK)
        deal_w2(1)
        for a in range(2):
            quantise_w1(0, a)
        for j0, n, tag in ((HALF, EARLY, "early"), (HALF + EARLY, HALF - EARLY, "picks1")):
            picks = picks_tile(n, tag)
            for i in range(PACK):
                gather(picks, 0, 1, i, j0, n)
            quantise_x(weave_x(nc.vector.tensor_copy, picks, 0, n), 1, j0, n)
        quantise_x(xb0[1], 0, HALF, HALF)

        hq = [keep.tile([P, S], U32, name="hq%d" % blk, align_bytes=64) for blk in range(2)]
        hs = [keep.tile([P, S], U8, name="hs%d" % blk, align_bytes=64) for blk in range(2)]
        groups = [(blk, half) for half in range(2) for blk in range(2)]
        last_group = len(groups) - 1
        mags = {}

        def b_pass(bank, blk, a, t, cols, start, stop):
            nc.tensor.matmul_mx(
                out=bank,
                lhsT=w2[blk][:, a, 2 * t * P : 2 * (t + 1) * P].bitcast(FP4X4),
                lhsT_scale=s2[blk][:, a, t * P : (t + 1) * P],
                rhs=xq[a][:, cols].bitcast(FP8X4),
                rhs_scale=xs[a][:, cols],
                start=start,
                stop=stop,
            )

        def damping_chunk(j0):
            if j0 == 0:
                mags[0] = keep.tile([P, HALF, PACK], F32, name="mag", tag="spare0")
            bank = psum.tile([P, PACK, CHUNK], F32, name="b_bank", bufs=B_BANKS)
            for a in range(2):
                for t in range(PACK):
                    first, final = (a, t) == (0, 0), (a, t) == (1, PACK - 1)
                    b_pass(bank[:, t, :], 0, a, t, slice(j0, j0 + CHUNK), first, final)
            nc.scalar.activation(
                out=mags[0][:, j0 : j0 + CHUNK, :], in_=bank[:].rearrange("p t n -> p n t"), func=ACT.Abs
            )

        def damping_wide(g, t):
            blk, half = groups[g]
            if t == 0:
                mags[g] = keep.tile([P, PACK, HALF], F32, name="mag", tag="spare%d" % (g % 2))
            bank = psum.tile([P, HALF], F32, name="b_bank", bufs=B_BANKS)
            for a in range(2):
                b_pass(bank[:], blk, a, t, slice(half * HALF, (half + 1) * HALF), a == 0, a == 1)
            nc.scalar.activation(out=mags[g][:, t, :], in_=bank[:], func=ACT.Abs)

        def inverse_root(g, j0, n):
            root = ring.tile([P, n, PACK], F32, name="root")
            if g == 0:
                dst = root[:].rearrange("p n t -> p (n t)")
                src = mags[0][:, j0 : j0 + n, :].rearrange("p n t -> p (n t)")
            else:
                dst = root[:].rearrange("p (c e) t -> p c t e", e=PAIR)
                src = mags[g][:, :, j0 : j0 + n].rearrange("p t (c e) -> p c t e", e=PAIR)
            nc.scalar.activation(out=dst, in_=src, func=ACT.Abs_reciprocal_sqrt, bias=one)
            return root

        def reciprocal(root, g, j0, n):
            recip = ring.tile([P, n, PACK], F32, name="recip", bufs=RECIP_BUFS)
            if 0 < g < last_group and j0 + n == HALF:
                nc.vector.tensor_tensor(recip[:], root[:], root[:], ALU.mult)
            else:
                nc.scalar.activation(out=recip[:], in_=root[:], func=ACT.Square)
            return recip

        def signal(recip, g, j0, n):
            blk, half = groups[g]
            hb = ring.tile([P, n, PACK], BF16, name="hb", align_bytes=64)
            for c0 in range(0, n, CHUNK):
                cols = slice(half * HALF + j0 + c0, half * HALF + j0 + c0 + CHUNK)
                bank = psum.tile([P, PACK, CHUNK], F32, name="a_bank", bufs=A_BANKS)
                for t in range(PACK):
                    for a in range(2):
                        nc.tensor.matmul_mx(
                            out=bank[:, t, :],
                            lhsT=w1q[blk, a][:, t * P : (t + 1) * P].bitcast(FP8X4),
                            lhsT_scale=w1s[blk, a][:, t * P : (t + 1) * P],
                            rhs=xq[a][:, cols].bitcast(FP8X4),
                            rhs_scale=xs[a][:, cols],
                            start=(a == 0),
                            stop=(a == 1),
                        )
                nc.vector.tensor_tensor(
                    hb[:, c0 : c0 + CHUNK, :],
                    bank[:].rearrange("p t n -> p n t"),
                    recip[:, c0 : c0 + CHUNK, :],
                    ALU.mult,
                )
            return hb

        def quantise_h(hb, g, j0, n):
            blk, half = groups[g]
            cols = slice(half * HALF + j0, half * HALF + j0 + n)
            quantise(hb, hq[blk][:, cols], hs[blk][:, cols])

        def y_pass(bank, blk, nt, cols, start, stop):
            nc.tensor.matmul_mx(
                out=bank,
                lhsT=w3[:, blk, nt * P : (nt + 1) * P].bitcast(FP8X4),
                lhsT_scale=s3[:, blk, nt * P : (nt + 1) * P],
                rhs=hq[blk][:, cols].bitcast(FP8X4),
                rhs_scale=hs[blk][:, cols],
                start=start,
                stop=stop,
            )

        def traits_wide(nt):
            bank = psum.tile([P, HALF], F32, name="y_bank", bufs=Y_BANKS)
            for blk in range(2):
                y_pass(bank[:], blk, nt, slice(0, HALF), blk == 0, blk == 1)
            res = big.tile([P, HALF], F32, name="res", tag="big")
            nc.vector.tensor_scalar(out=res[:], in0=bank[:], scalar1=bias[:, nt : nt + 1], scalar2=None, op0=ALU.add)
            nc.sync.dma_start(out=out[nt * P : (nt + 1) * P, 0:HALF], in_=res[:])

        def traits_rows(bank, j0, nt0, count, on_scalar):
            cols = slice(j0, j0 + CHUNK)
            for blk in range(2):
                for k in range(count):
                    y_pass(bank[:, k, :], blk, nt0 + k, cols, (blk, k) == (0, 0), (blk, k) == (1, count - 1))
            res = big.tile([P, count, CHUNK], F32, name="res", tag="big")
            if on_scalar:
                for k in range(count):
                    nc.scalar.activation(
                        out=res[:, k, :], in_=bank[:, k, :], func=ACT.Identity, bias=bias[:, nt0 + k : nt0 + k + 1]
                    )
            else:
                rows_bias = bias[:, nt0 : nt0 + count].unsqueeze(2).to_broadcast([P, count, CHUNK])
                nc.vector.tensor_tensor(res[:], bank[:], rows_bias, ALU.add)
            nc.sync.dma_start(
                out=out[nt0 * P : (nt0 + count) * P, cols].rearrange("(c p) j -> p c j", p=P), in_=res[:]
            )

        def traits_chunk(j0):
            if j0 == HALF:
                bank = psum.tile([P, N_TILES, CHUNK], F32, name="y_bank", bufs=Y_BANKS)
                traits_rows(bank, j0, 0, N_TILES, True)
            else:
                count = N_TILES // 2
                bank = psum.tile([P, count, CHUNK], F32, name="y_bank", bufs=Y_BANKS)
                traits_rows(bank, j0, 0, count, False)
                bank = psum.tile([P, count, CHUNK], F32, name="b_bank", bufs=B_BANKS)
                traits_rows(bank, j0, count, count, True)

        steps = [(g, j0, n) for g, n in enumerate(STEP_TOKENS) for j0 in range(0, HALF, n)]
        roots = {}

        def make_root(step):
            g, j0, n = step
            if step not in roots:
                if g == 0:
                    damping_chunk(j0)
                roots[step] = inverse_root(g, j0, n)

        before = None
        for step in steps:
            g, j0, n = step
            share = range(j0 // CHUNK, (j0 + n) // CHUNK)
            make_root(step)
            if j0 + n < HALF:
                make_root((g, j0 + n, n))
            recip = reciprocal(roots[step], g, j0, n)
            if g < last_group:
                for t in share:
                    damping_wide(g + 1, t)
            if before is None:
                for a in range(2):
                    quantise_w1(1, a)
            hb = signal(recip, g, j0, n)
            if before is not None:
                quantise_h(*before)
            before = (hb, g, j0, n)
            if g == last_group - 1:
                for nt in share:
                    traits_wide(nt)
            if g == last_group and j0 > 0:
                traits_chunk(HALF + j0 - CHUNK)
        quantise_h(*before)
        traits_chunk(S - CHUNK)
